import numpy as np
import ml_dtypes


def mxq(x, axis, fmt="e4m3"):
    dtype, down = {"e4m3": (ml_dtypes.float8_e4m3fn, 7), "e5m2": (ml_dtypes.float8_e5m2, 14)}[fmt]
    v = np.moveaxis(np.asarray(x, np.float32).astype(ml_dtypes.bfloat16).astype(np.float64), axis, -1)
    blocks = v.reshape(v.shape[:-1] + (-1, 32))
    amax = np.abs(blocks).max(-1, keepdims=True)
    byte = np.maximum(np.where(amax > 0, np.frexp(amax)[1] - 1 + 127, 0) - down, 1)
    scale = np.exp2(byte - 127.0)
    codes = (blocks / scale).astype(np.float32).astype(dtype).astype(np.float64)
    return np.moveaxis((codes * scale).reshape(v.shape), -1, axis)


WIDE = False


def mx_kscale(k):
    if not WIDE:
        return np.ones(k)
    levels = np.array([10, -10, 5, -5, 0])
    if k % 512:
        return np.exp2(np.random.permutation(np.resize(levels, k // 32))).repeat(32)
    a = np.empty((k // 512, 16))
    for p in range(k // 512):
        a[p, :8] = np.random.permutation(np.resize(levels, 8))
        for g in range(8):
            far = levels[np.abs(levels - a[p, g]) >= 10]
            a[p, g + 8] = far[np.random.randint(len(far))]
    return np.exp2(a.ravel()).repeat(32)


def f64(x):
    return np.asarray(x).astype(np.float64)


def striped(idx):
    return np.tile(idx.reshape(-1, 16).T, (8, 1)).astype(np.uint16)


def unstriped(offs):
    return offs[:16].T.reshape(-1).astype(np.int64)


E2M1 = np.array([0.0, 0.5, 1.0, 1.5, 2.0, 3.0, 4.0, 6.0, -0.0, -0.5, -1.0, -1.5, -2.0, -3.0, -4.0, -6.0])


def pack_weight(w, fmt):
    k, n = w.shape
    w = f64(np.asarray(w, np.float32).astype(ml_dtypes.bfloat16)).reshape(k // 32, 32, n)
    amax = np.abs(w).max(1)
    if fmt == "e4m3":
        byte = np.frexp(amax)[1] - 1 + 127 - 7
    else:
        mant, ex = np.frexp(amax / 6.0)
        byte = np.where(mant > 0.5, ex, ex - 1) + 127
    byte = np.clip(np.where(amax > 0, byte, 1), 1, 254)
    scaled = (w * np.exp2(127.0 - byte)[:, None, :]).reshape(k, n).astype(np.float32)
    by_word = np.ascontiguousarray(scaled.reshape(k // 512, 128, 4, n).transpose(0, 1, 3, 2))
    if fmt == "e4m3":
        words = by_word.astype(ml_dtypes.float8_e4m3fn).view(np.uint8)
    else:
        c = by_word.astype(ml_dtypes.float4_e2m1fn).view(np.uint8) & 0xF
        words = (c[..., 0::2] | (c[..., 1::2] << 4)).reshape(k // 512, 128, 2 * n)
    return np.ascontiguousarray(words), np.ascontiguousarray(byte.astype(np.uint8).reshape(k // 512, 16, n))


def unpack_weight(words, scales, fmt):
    g, _, n = scales.shape
    words = np.ascontiguousarray(words).reshape(g, 128, n, -1)
    if fmt == "e4m3":
        vals = words.view(ml_dtypes.float8_e4m3fn).astype(np.float64)
    else:
        nib = np.empty((g, 128, n, 4), np.uint8)
        nib[..., 0::2] = words & 0xF
        nib[..., 1::2] = words >> 4
        vals = E2M1[nib]
    vals = vals * np.repeat(np.exp2(scales.astype(np.float64) - 127.0), 8, axis=1)[..., None]
    return vals.transpose(0, 1, 3, 2).reshape(g * 512, n)


def gelu(v):
    return 0.5 * v * (1.0 + np.tanh(np.sqrt(2.0 / np.pi) * (v + 0.044715 * v**3)))


def often(T, S):
    return np.random.permutation(T)[(T * np.random.uniform(0, 1, S) ** 4).astype(np.int64)]


K, K2, H, T, S, P = 1024, 512, 1024, 4096, 1024, 512

def setup_inputs():
    n = np.random.standard_normal
    s, s2, s3 = mx_kscale(K)[:, None], mx_kscale(K2)[:, None], mx_kscale(K2)[:, None]
    u = mx_kscale(H)[:, None]
    d = {}
    d["tab_words"], d["tab_scales"] = pack_weight(n((K, T)) * s, "e4m3")
    d["tab2_words"], d["tab2_scales"] = pack_weight(n((K2, T)) * s2, "e4m3")
    d["tab3_words"], d["tab3_scales"] = pack_weight(n((K2, T)) * s3, "e4m3")
    d["offs"] = striped(np.random.permutation(T)[:S])
    d["offs2"] = striped(np.random.permutation(T)[:S])
    d["offs3"] = striped(np.random.permutation(T)[:S])
    d["pos1"] = striped(np.random.permutation(S)[:P])
    d["pos2"] = striped(often(S, P))
    d["pos3"] = striped(often(S, P))
    d["w1"] = (n((K, H)) / K**0.5 / s).astype(np.float32)
    d["w2_words"], d["w2_scales"] = pack_weight(n((K2, H)) / K2**0.5 / s2, "e2m1")
    d["w3"] = (n((K2, H)) / K2**0.5 / s3 * u.T).astype(np.float32)
    d["w4_words"], d["w4_scales"] = pack_weight(n((H, H)) / H**0.5 / u, "e2m1")
    d["draw"] = np.exp(0.3 * n(H)).astype(np.float32)
    d["fit"] = (1.2 * np.exp(0.3 * n(H)) * u[:, 0]).astype(np.float32)
    d["lim"] = (np.exp(0.3 * n(H)) / u[:, 0]).astype(np.float32)
    return d

def reference(tab_words, tab_scales, tab2_words, tab2_scales, tab3_words, tab3_scales, offs, offs2, offs3,
              pos1, pos2, pos3, w1, w2_words, w2_scales, w3, w4_words, w4_scales, draw, fit, lim):
    v = unpack_weight(tab_words, tab_scales, "e4m3")[:, unstriped(offs)]
    v2 = unpack_weight(tab2_words, tab2_scales, "e4m3")[:, unstriped(offs2)]
    v3 = unpack_weight(tab3_words, tab3_scales, "e4m3")[:, unstriped(offs3)]
    a = mxq(f64(w1), 0, "e4m3").T @ v
    b = unpack_weight(w2_words, w2_scales, "e2m1").T @ v2
    d = mxq(f64(w3), 0, "e4m3").T @ v3
    a1 = a[:, unstriped(pos1)]
    b1 = b[:, unstriped(pos2)]
    d1 = d[:, unstriped(pos3)]
    t = np.tanh(f64(draw)[:, None] * a1 - b1)
    z = f64(fit)[:, None] * t + d1
    y = unpack_weight(w4_words, w4_scales, "e2m1").T @ mxq(z, 0, "e4m3")
    return np.minimum(y, f64(lim)[:, None] * d1)

@@ -1,0 +1,295 @@
+from contextlib import ExitStack
+
+import concourse.mybir as mybir
+
+K, K2, H, T, S, PICK = 1024, 512, 1024, 4096, 1024, 512
+FLOPS = 2 * H * S * (K + K2 + K2) + 2 * H * H * PICK
+
+F32 = mybir.dt.float32
+BF16 = mybir.dt.bfloat16
+I32 = mybir.dt.int32
+U32 = mybir.dt.uint32
+U16 = mybir.dt.uint16
+U8 = mybir.dt.uint8
+FP8X4 = mybir.dt.float8_e4m3fn_x4
+FP4X4 = mybir.dt.float4_e2m1fn_x4
+ALU = mybir.AluOpType
+ACT = mybir.ActivationFunctionType
+
+P = 128
+PACK = 4
+K_PASS = P * PACK
+BANK = 512
+BLOCKS = H // K_PASS
+ROW_TILES = [(blk, i) for blk in range(BLOCKS) for i in range(PACK)]
+
+
+def tile_list_cinema_week_scores_kernel(
+    tc, tab_words, tab_scales, tab2_words, tab2_scales, tab3_words, tab3_scales, offs, offs2, offs3,
+    pos1, pos2, pos3, w1, w2_words, w2_scales, w3, w4_words, w4_scales, draw, fit, lim, out,
+):
+    nc = tc.nc
+    with ExitStack() as ctx:
+        lists = ctx.enter_context(tc.tile_pool(name="lists", bufs=1))
+        keep = ctx.enter_context(tc.tile_pool(name="keep", bufs=1))
+        ring = ctx.enter_context(tc.tile_pool(name="ring", bufs=1))
+        psum = ctx.enter_context(tc.psum_pool(name="psum", bufs=1))
+
+        def turns(pool, name, count, shape, dtype):
+            tiles = [pool.tile(shape, dtype, name="%s%d" % (name, n), tag="%s%d" % (name, n)) for n in range(count)]
+
+            def take():
+                tiles.append(tiles.pop(0))
+                return tiles[-1]
+
+            return take
+
+        bank = turns(psum, "bank", 8, [P, BANK], F32)
+        window = turns(ring, "window", 4, [P, S], F32)
+        late_window = turns(ring, "late_window", 4, [P, S], F32)
+        scratch = turns(ring, "scratch", 8, [P, PICK], F32)
+        float_weight = turns(ring, "float_weight", 4, [P, PACK, K_PASS], F32)
+        slots = {name: ring.tile([P, 2 * PICK], F32, name="slot_" + name, align_bytes=64) for name in "abcd"}
+
+        def load_list(name, src):
+            tile = lists.tile([P, src.shape[1]], U16, name=name)
+            nc.sync.dma_start(tile[:], src)
+            return tile
+
+        def load_channel_vector(name, src):
+            tile = keep.tile([P, BLOCKS, PACK], F32, name=name)
+            nc.sync.dma_start(tile[:], src.rearrange("(b p i) -> p b i", p=P, i=PACK))
+            return tile
+
+        def zeroed_bytes(name, shape, engine, partitions=P):
+            tile = keep.tile(shape, U8, name=name, tag=name, align_bytes=64)
+            engine.memset(tile[0:partitions].bitcast(I32), 0)
+            return tile
+
+        def load_scale_rows(tile, src, first):
+            rows = src.rearrange("g q n -> (g q) n")
+            nc.sync.dma_start(tile[first : first + rows.shape[0], :].bitcast(I32), rows.bitcast(I32))
+
+        def place_scale_rows(plane, rows, first_row, first_partition=0):
+            for r in range(4):
+                nc.sync.dma_start(
+                    plane[first_partition + r : P : 32, :].bitcast(I32),
+                    rows[first_row + r : first_row + 16 : 4, :].bitcast(I32),
+                )
+
+        def load_planes(planes, src, queue):
+            for r in range(4):
+                queue.dma_start(planes[r:P:32, :, :].bitcast(I32), src[:, r:16:4, :].rearrange("g q n -> q g n").bitcast(I32))
+
+        def deal_fp4_planes(name, planes):
+            passes = planes.shape[1]
+            dealt = keep.tile([P, passes, H], U8, name=name, align_bytes=64)
+            nc.vector.tensor_copy(
+                dealt[:].rearrange("p g (b i m) -> p (g b) i m", b=BLOCKS, i=PACK),
+                planes[:].rearrange("p g (b m i) -> p (g b) i m", b=BLOCKS, i=PACK),
+            )
+            return dealt
+
+        def load_table_words(name, src, tag):
+            tile = ring.tile([P, T], I32, name=name, tag=tag)
+            nc.sync.dma_start(tile[:], src.rearrange("p n i -> p (n i)").bitcast(I32))
+            return tile
+
+        def load_fp4_words(name, src, tag):
+            tile = ring.tile([P, src.shape[0], H // 2], I32, name=name, tag=tag)
+            nc.sync.dma_start(tile[:], src.rearrange("g p n -> p g n").bitcast(I32))
+            return tile
+
+        def load_float_weight(w, g, blk):
+            tile = float_weight()
+            rows = w[g * K_PASS : (g + 1) * K_PASS, blk * K_PASS : (blk + 1) * K_PASS]
+            nc.sync.dma_start(tile[:], rows.rearrange("(p j) c -> p j c", j=PACK))
+            return tile
+
+        def gather_words(name, table, offsets):
+            tile = keep.tile([P, S], U32, name=name, align_bytes=64)
+            nc.vector.tensor_copy(tile[:], table[:].bitcast(U32).indirect(offsets[:]))
+            return tile
+
+        def gather_scales(name, plane, offsets):
+            tile = keep.tile([P, S], U8, name=name, align_bytes=64)
+            nc.vector.tensor_copy(tile[:], plane[:].indirect(offsets[:]))
+            return tile
+
+        def round_weight(raw, copy, slot):
+            tile = slots[slot][:].bitcast(BF16)
+            copy(tile[:].rearrange("p (i m j) -> p m i j", i=PACK, j=PACK), raw[:].rearrange("p j (m i) -> p m i j", i=PACK))
+            return tile
+
+        def quantize(name, rounded):
+            codes = keep.tile([P, K_PASS], U32, name=name + "_codes", align_bytes=64)
+            scales = keep.tile([P, K_PASS], U8, name=name + "_scales", align_bytes=64)
+            nc.vector.quantize_mx(out=codes[:].bitcast(FP8X4), scales=scales[:], in_=rounded[:])
+            return codes, scales
+
+        def deal_fp4_words(name, words):
+            passes = words.shape[1]
+            dealt = keep.tile([P, passes, 2 * H], U8, name=name, align_bytes=64)
+            for g in range(passes):
+                nc.scalar.copy(
+                    dealt[:, g, :].bitcast(U16).rearrange("p (b i m) -> p b i m", b=BLOCKS, i=PACK),
+                    words[:, g, :].bitcast(U16).rearrange("p (b m i) -> p b i m", b=BLOCKS, i=PACK),
+                )
+            return dealt
+
+        def fp8_side(quantized, blk, i):
+            cols = slice(i * P, (i + 1) * P)
+            return [(q[blk][0][:, cols].bitcast(FP8X4), q[blk][1][:, cols]) for q in quantized]
+
+        def fp4_side(dealt, blk, i):
+            c0 = blk * K_PASS + i * P
+            return [
+                (dealt[0][:, g, 2 * c0 : 2 * (c0 + P)].bitcast(FP4X4), dealt[1][:, g, c0 : c0 + P])
+                for g in range(dealt[0].shape[1])
+            ]
+
+        def first_stage(rows, stationary, moving):
+            for c0 in range(0, S, BANK):
+                acc = bank()
+                for g, ((w_codes, w_scales), (v_words, v_plane, first)) in enumerate(zip(stationary, moving)):
+                    nc.tensor.matmul_mx(
+                        out=acc[:], lhsT=w_codes, lhsT_scale=w_scales,
+                        rhs=v_words[:, c0 : c0 + BANK].bitcast(FP8X4), rhs_scale=v_plane[first:P, c0 : c0 + BANK],
+                        start=(g == 0), stop=(g == len(moving) - 1),
+                    )
+                nc.scalar.copy(rows[:, c0 : c0 + BANK], acc[:])
+            return rows
+
+        w2_planes = zeroed_bytes("w2_planes", [P, 1, H], nc.vector)
+        rows2 = zeroed_bytes("rows2", [P, T], nc.vector, P - 16)
+        rows3 = zeroed_bytes("rows3", [P, T], nc.vector, P - 16)
+        rows1 = zeroed_bytes("rows1", [P, T], nc.gpsimd)
+        planes23 = zeroed_bytes("planes23", [P, 2 * S], nc.gpsimd)
+        w4_planes = zeroed_bytes("w4_planes", [P, 2, H], nc.gpsimd)
+
+        list2 = load_list("list2", offs2)
+        load_scale_rows(rows2, tab2_scales, P - 16)
+        list3 = load_list("list3", offs3)
+        load_scale_rows(rows3, tab3_scales, P - 16)
+        w2_packed = load_fp4_words("w2_packed", w2_words, "w2_packed")
+        pick2 = load_list("pick2", pos2)
+        draw_t = load_channel_vector("draw_t", draw)
+        table2 = load_table_words("table2", tab2_words[0], "table_a")
+        load_planes(w2_planes, w2_scales, nc.sync)
+
+        picked23 = keep.tile([P, 2 * S], U8, name="picked23")
+        nc.vector.tensor_copy(picked23[:, 0:S], rows2[:].indirect(list2[:]))
+        nc.vector.tensor_copy(picked23[:, S : 2 * S], rows3[:].indirect(list3[:]))
+        place_scale_rows(planes23, picked23, P - 16)
+        plane2, plane3 = planes23[:, 0:S], planes23[:, S : 2 * S]
+        w3_raw = [load_float_weight(w3, 0, 0)]
+        list1 = load_list("list1", offs)
+        pick3 = load_list("pick3", pos3)
+        table3 = load_table_words("table3", tab3_words[0], "table_b")
+        for q in range(4):
+            nc.sync.dma_start(rows1[32 * q : 32 * q + 8, :].bitcast(I32), tab_scales[:, 4 * q : 4 * q + 4, :].bitcast(I32))
+        w3_raw.append(load_float_weight(w3, 0, 1))
+        table1 = [load_table_words("table1_0", tab_words[0], "table_c"), load_table_words("table1_1", tab_words[1], "table_a")]
+        w1_raw = {(g, 0): load_float_weight(w1, g, 0) for g in range(2)}
+        pick1 = load_list("pick1", pos1)
+        fit_t = load_channel_vector("fit_t", fit)
+        load_planes(w4_planes, w4_scales, nc.sync)
+        lim_t = load_channel_vector("lim_t", lim)
+
+        words2 = gather_words("words2", table2, list2)
+        w2_dealt = (deal_fp4_words("w2_dealt", w2_packed), deal_fp4_planes("w2_dealt_planes", w2_planes))
+        w3_q = [quantize("w3_0", round_weight(w3_raw[0], nc.vector.tensor_copy, "a"))]
+
+        draw_wide = keep.tile([P, PACK, PICK], F32, name="draw_wide")
+        nc.scalar.copy(draw_wide[:], draw_t[:, 1, :].unsqueeze(2).to_broadcast([P, PACK, PICK]))
+
+        def picked(name, rows, offsets):
+            tile = keep.tile([P, PICK], F32, name=name)
+            nc.vector.tensor_copy(tile[:], rows[:].indirect(offsets[:]))
+            return tile
+
+        def pick_audiences(blk, pairs, windows):
+            for half, pair in enumerate(pairs):
+                for e in range(2):
+                    d_rows = first_stage(windows[2 * half + e], fp8_side([w3_q], blk, 2 * half + e), [(words3, plane3, 0)])
+                    nc.vector.tensor_copy(pair[:, e * PICK : (e + 1) * PICK], d_rows[:].indirect(pick3[:]))
+                    d_picked[blk, 2 * half + e] = pair[:, e * PICK : (e + 1) * PICK]
+
+        def film_rows(blk, i):
+            return first_stage(window(), fp8_side(w1_q, blk, i), [(words1[g], plane1, 4 * g) for g in range(2)])
+
+        def join(z_rows, blk, i, gap, sign):
+            match = scratch()
+            nc.scalar.activation(match[:], gap[:], ACT.Tanh, scale=sign)
+            nc.vector.scalar_tensor_tensor(
+                z_rows[:, i, :], match[:], fit_t[:, blk, i : i + 1], d_picked[blk, i], ALU.mult, ALU.add
+            )
+
+        def weave(name, z_rows, copy, slot):
+            z_woven = slots[slot][:].bitcast(BF16)
+            copy(z_woven[:].rearrange("p (c e i) -> p c i e", e=4, i=PACK), z_rows[:].rearrange("p i (c e) -> p c i e", e=4))
+            return quantize(name, z_woven)
+
+        b_picked = []
+        for i in range(PACK):
+            b_rows = first_stage(window(), fp4_side(w2_dealt, 0, i), [(words2, plane2, 0)])
+            b_picked.append(picked("b_picked%d" % i, b_rows, pick2))
+        words3 = gather_words("words3", table3, list3)
+        plane1 = gather_scales("plane1", rows1, list1)
+        d_picked = {}
+        b_late = [first_stage(late_window(), fp4_side(w2_dealt, 1, i), [(words2, plane2, 0)]) for i in range(PACK)]
+        pick_audiences(0, [keep.tile([P, 2 * PICK], F32, name="d_pair%d" % n) for n in range(2)], [window() for i in range(PACK)])
+        w3_q.append(quantize("w3_1", round_weight(w3_raw[1], nc.scalar.copy, "b")))
+        for g in range(2):
+            w1_raw[g, 1] = load_float_weight(w1, g, 1)
+        words1 = [gather_words("words1_%d" % g, table1[g], list1) for g in range(2)]
+        w1_q = [
+            [quantize("w1_00", round_weight(w1_raw[0, 0], nc.scalar.copy, "a"))],
+            [quantize("w1_10", round_weight(w1_raw[1, 0], nc.vector.tensor_copy, "b"))],
+        ]
+        d_windows = [ring.tile([P, 2 * S], F32, name="d_windows%d" % n, tag="float_weight%d" % (2 + n)) for n in range(2)]
+        pick_audiences(1, [slots["a"], slots["b"]], [d_windows[i // 2][:, (i % 2) * S : (i % 2 + 1) * S] for i in range(PACK)])
+
+        z_rows0 = keep.tile([P, PACK, PICK], BF16, name="z_rows0", tag="rows2", align_bytes=64)
+        a_rows = [film_rows(0, i) for i in range(PACK)]
+        w1_q[0].append(quantize("w1_01", round_weight(w1_raw[0, 1], nc.scalar.copy, "c")))
+        for i in range(PACK):
+            if i < PACK - 1:
+                a_picked = scratch()
+            else:
+                a_picked = slots["d"][:, 0:PICK]
+            nc.vector.tensor_copy(a_picked[:], a_rows[i][:].indirect(pick1[:]))
+            gap = scratch()
+            nc.vector.scalar_tensor_tensor(gap[:], a_picked[:], draw_t[:, 0, i : i + 1], b_picked[i][:], ALU.mult, ALU.subtract)
+            join(z_rows0, 0, i, gap, 1.0)
+            if i == 0:
+                w1_q[1].append(quantize("w1_11", round_weight(w1_raw[1, 1], nc.scalar.copy, "d")))
+
+        w4_packed = load_fp4_words("w4_packed", w4_words, "float_weight1")
+        z_rows1 = keep.tile([P, PACK, PICK], BF16, name="z_rows1", tag="rows3", align_bytes=64)
+        a_rows = [film_rows(1, i) for i in range(PACK)]
+        z_q = [weave("z0", z_rows0, nc.scalar.copy, "c")]
+        w4_dealt = (deal_fp4_words("w4_dealt", w4_packed), deal_fp4_planes("w4_dealt_planes", w4_planes))
+        for i in range(PACK):
+            drawn = scratch()
+            nc.vector.tensor_tensor(drawn[:], a_rows[i][:].indirect(pick1[:]), draw_wide[:, i, :], ALU.mult)
+            gap = scratch()
+            nc.vector.tensor_tensor(gap[:], b_late[i][:].indirect(pick2[:]), drawn[:], ALU.subtract)
+            join(z_rows1, 1, i, gap, -1.0)
+        z_q.append(weave("z1", z_rows1, nc.vector.tensor_copy, "d"))
+
+        out_rows = out.rearrange("(b p i) j -> b i p j", p=P, i=PACK)
+        y_acc = {key: bank() for key in ROW_TILES}
+        for g in range(BLOCKS):
+            for blk, i in ROW_TILES:
+                w_codes, w_scales = fp4_side(w4_dealt, blk, i)[g]
+                nc.tensor.matmul_mx(
+                    out=y_acc[blk, i][:], lhsT=w_codes, lhsT_scale=w_scales,
+                    rhs=z_q[g][0][:].bitcast(FP8X4), rhs_scale=z_q[g][1][:], start=(g == 0), stop=(g == BLOCKS - 1),
+                )
+        for blk, i in ROW_TILES:
+            limited = scratch()
+            nc.vector.scalar_tensor_tensor(
+                limited[:], d_picked[blk, i], lim_t[:, blk, i : i + 1], y_acc[blk, i][:], ALU.mult, ALU.min
+            )
+            nc.sync.dma_start(out_rows[blk, i], limited[:])

@@ -21,6 +21,7 @@ PACK = 4
 K_PASS = P * PACK
 BANK = 512
 BLOCKS = H // K_PASS
+EARLY = 2
 ROW_TILES = [(blk, i) for blk in range(BLOCKS) for i in range(PACK)]
 
 
@@ -35,8 +36,8 @@ def tile_list_cinema_week_scores_kernel(
         ring = ctx.enter_context(tc.tile_pool(name="ring", bufs=1))
         psum = ctx.enter_context(tc.psum_pool(name="psum", bufs=1))
 
-        def turns(pool, name, count, shape, dtype):
-            tiles = [pool.tile(shape, dtype, name="%s%d" % (name, n), tag="%s%d" % (name, n)) for n in range(count)]
+        def turns(pool, name, count, shape, dtype, align=64):
+            tiles = [pool.tile(shape, dtype, name="%s%d" % (name, n), tag="%s%d" % (name, n), align_bytes=align) for n in range(count)]
 
             def take():
                 tiles.append(tiles.pop(0))
@@ -44,12 +45,12 @@ def tile_list_cinema_week_scores_kernel(
 
             return take
 
-        bank = turns(psum, "bank", 8, [P, BANK], F32)
+        bank = turns(psum, "bank", 8, [P, BANK], F32, None)
         window = turns(ring, "window", 4, [P, S], F32)
         late_window = turns(ring, "late_window", 4, [P, S], F32)
         scratch = turns(ring, "scratch", 8, [P, PICK], F32)
         float_weight = turns(ring, "float_weight", 4, [P, PACK, K_PASS], F32)
-        slots = {name: ring.tile([P, 2 * PICK], F32, name="slot_" + name, align_bytes=64) for name in "abcd"}
+        slots = {name: ring.tile([P, 2 * PICK], F32, name="slot_" + name, align_bytes=64) for name in "abcde"}
 
         def load_list(name, src):
             tile = lists.tile([P, src.shape[1]], U16, name=name)
@@ -96,7 +97,7 @@ def tile_list_cinema_week_scores_kernel(
             return tile
 
         def load_fp4_words(name, src, tag):
-            tile = ring.tile([P, src.shape[0], H // 2], I32, name=name, tag=tag)
+            tile = ring.tile([P, src.shape[0], H // 2], I32, name=name, tag=tag, align_bytes=64)
             nc.sync.dma_start(tile[:], src.rearrange("g p n -> p g n").bitcast(I32))
             return tile
 
@@ -127,9 +128,9 @@ def tile_list_cinema_week_scores_kernel(
             nc.vector.quantize_mx(out=codes[:].bitcast(FP8X4), scales=scales[:], in_=rounded[:])
             return codes, scales
 
-        def deal_fp4_words(name, words):
+        def deal_fp4_words(name, words, tag):
             passes = words.shape[1]
-            dealt = keep.tile([P, passes, 2 * H], U8, name=name, align_bytes=64)
+            dealt = ring.tile([P, passes, 2 * H], U8, name=name, tag=tag, align_bytes=64)
             for g in range(passes):
                 nc.scalar.copy(
                     dealt[:, g, :].bitcast(U16).rearrange("p (b i m) -> p b i m", b=BLOCKS, i=PACK),
@@ -163,7 +164,8 @@ def tile_list_cinema_week_scores_kernel(
         w2_planes = zeroed_bytes("w2_planes", [P, 1, H], nc.vector)
         rows2 = zeroed_bytes("rows2", [P, T], nc.vector, P - 16)
         rows3 = zeroed_bytes("rows3", [P, T], nc.vector, P - 16)
-        rows1 = zeroed_bytes("rows1", [P, T], nc.gpsimd)
+        rows1 = zeroed_bytes("rows1", [P, T], nc.gpsimd, P - 32)
+        plane1 = zeroed_bytes("plane1", [P, S], nc.gpsimd)
         planes23 = zeroed_bytes("planes23", [P, 2 * S], nc.gpsimd)
         w4_planes = zeroed_bytes("w4_planes", [P, 2, H], nc.gpsimd)
 
@@ -171,25 +173,28 @@ def tile_list_cinema_week_scores_kernel(
         load_scale_rows(rows2, tab2_scales, P - 16)
         list3 = load_list("list3", offs3)
         load_scale_rows(rows3, tab3_scales, P - 16)
+        list1 = load_list("list1", offs)
+        load_scale_rows(rows1, tab_scales, P - 32)
         w2_packed = load_fp4_words("w2_packed", w2_words, "w2_packed")
-        pick2 = load_list("pick2", pos2)
-        draw_t = load_channel_vector("draw_t", draw)
         table2 = load_table_words("table2", tab2_words[0], "table_a")
         load_planes(w2_planes, w2_scales, nc.sync)
+        draw_t = load_channel_vector("draw_t", draw)
+        w3_raw = [load_float_weight(w3, 0, 0)]
+        pick2 = load_list("pick2", pos2)
 
         picked23 = keep.tile([P, 2 * S], U8, name="picked23")
         nc.vector.tensor_copy(picked23[:, 0:S], rows2[:].indirect(list2[:]))
         nc.vector.tensor_copy(picked23[:, S : 2 * S], rows3[:].indirect(list3[:]))
         place_scale_rows(planes23, picked23, P - 16)
         plane2, plane3 = planes23[:, 0:S], planes23[:, S : 2 * S]
-        w3_raw = [load_float_weight(w3, 0, 0)]
-        list1 = load_list("list1", offs)
-        pick3 = load_list("pick3", pos3)
+        picked1 = gather_scales("picked1", rows1, list1)
         table3 = load_table_words("table3", tab3_words[0], "table_b")
-        for q in range(4):
-            nc.sync.dma_start(rows1[32 * q : 32 * q + 8, :].bitcast(I32), tab_scales[:, 4 * q : 4 * q + 4, :].bitcast(I32))
+        pick3 = load_list("pick3", pos3)
         w3_raw.append(load_float_weight(w3, 0, 1))
-        table1 = [load_table_words("table1_0", tab_words[0], "table_c"), load_table_words("table1_1", tab_words[1], "table_a")]
+        place_scale_rows(plane1, picked1, P - 32)
+        table1 = [load_table_words("table1_0", tab_words[0], "table_c")]
+        place_scale_rows(plane1, picked1, P - 16, 4)
+        table1.append(load_table_words("table1_1", tab_words[1], "table_a"))
         w1_raw = {(g, 0): load_float_weight(w1, g, 0) for g in range(2)}
         pick1 = load_list("pick1", pos1)
         fit_t = load_channel_vector("fit_t", fit)
@@ -197,16 +202,11 @@ def tile_list_cinema_week_scores_kernel(
         lim_t = load_channel_vector("lim_t", lim)
 
         words2 = gather_words("words2", table2, list2)
-        w2_dealt = (deal_fp4_words("w2_dealt", w2_packed), deal_fp4_planes("w2_dealt_planes", w2_planes))
-        w3_q = [quantize("w3_0", round_weight(w3_raw[0], nc.vector.tensor_copy, "a"))]
+        w2_dealt = (deal_fp4_words("w2_dealt", w2_packed, "w2_dealt"), deal_fp4_planes("w2_dealt_planes", w2_planes))
+        w3_q = [quantize("w3_0", round_weight(w3_raw[0], nc.vector.tensor_copy, "e"))]
 
-        draw_wide = keep.tile([P, PACK, PICK], F32, name="draw_wide")
-        nc.scalar.copy(draw_wide[:], draw_t[:, 1, :].unsqueeze(2).to_broadcast([P, PACK, PICK]))
-
-        def picked(name, rows, offsets):
-            tile = keep.tile([P, PICK], F32, name=name)
-            nc.vector.tensor_copy(tile[:], rows[:].indirect(offsets[:]))
-            return tile
+        draw_wide = keep.tile([P, PACK - EARLY, PICK], F32, name="draw_wide")
+        nc.scalar.copy(draw_wide[:], draw_t[:, 1, EARLY:].unsqueeze(2).to_broadcast([P, PACK - EARLY, PICK]))
 
         def pick_audiences(blk, pairs, windows):
             for half, pair in enumerate(pairs):
@@ -215,14 +215,21 @@ def tile_list_cinema_week_scores_kernel(
                     nc.vector.tensor_copy(pair[:, e * PICK : (e + 1) * PICK], d_rows[:].indirect(pick3[:]))
                     d_picked[blk, 2 * half + e] = pair[:, e * PICK : (e + 1) * PICK]
 
-        def film_rows(blk, i):
-            return first_stage(window(), fp8_side(w1_q, blk, i), [(words1[g], plane1, 4 * g) for g in range(2)])
+        def film_rows(blk, i, passes):
+            return first_stage(
+                window(), fp8_side([w1_q[g] for g in passes], blk, i), [(words1[g], plane1, 4 * g) for g in passes]
+            )
 
-        def join(z_rows, blk, i, gap, sign):
+        matches = {}
+
+        def tanh(gap, sign):
             match = scratch()
             nc.scalar.activation(match[:], gap[:], ACT.Tanh, scale=sign)
+            return match
+
+        def join(z_rows, blk, i):
             nc.vector.scalar_tensor_tensor(
-                z_rows[:, i, :], match[:], fit_t[:, blk, i : i + 1], d_picked[blk, i], ALU.mult, ALU.add
+                z_rows[:, i, :], matches[blk, i][:], fit_t[:, blk, i : i + 1], d_picked[blk, i], ALU.mult, ALU.add
             )
 
         def weave(name, z_rows, copy, slot):
@@ -230,52 +237,80 @@ def tile_list_cinema_week_scores_kernel(
             copy(z_woven[:].rearrange("p (c e i) -> p c i e", e=4, i=PACK), z_rows[:].rearrange("p i (c e) -> p c i e", e=4))
             return quantize(name, z_woven)
 
-        b_picked = []
-        for i in range(PACK):
-            b_rows = first_stage(window(), fp4_side(w2_dealt, 0, i), [(words2, plane2, 0)])
-            b_picked.append(picked("b_picked%d" % i, b_rows, pick2))
+        b_rows = [first_stage(window(), fp4_side(w2_dealt, 0, i), [(words2, plane2, 0)]) for i in range(PACK)]
         words3 = gather_words("words3", table3, list3)
-        plane1 = gather_scales("plane1", rows1, list1)
+        b_pairs = [slots["e"], ring.tile([P, 2 * PICK], F32, name="b_pair", tag="table_b")]
+        b_picked = [b_pairs[i // 2][:, (i % 2) * PICK : (i % 2 + 1) * PICK] for i in range(PACK)]
+        for i in range(PACK):
+            nc.vector.tensor_copy(b_picked[i], b_rows[i][:].indirect(pick2[:]))
         d_picked = {}
         b_late = [first_stage(late_window(), fp4_side(w2_dealt, 1, i), [(words2, plane2, 0)]) for i in range(PACK)]
         pick_audiences(0, [keep.tile([P, 2 * PICK], F32, name="d_pair%d" % n) for n in range(2)], [window() for i in range(PACK)])
         w3_q.append(quantize("w3_1", round_weight(w3_raw[1], nc.scalar.copy, "b")))
         for g in range(2):
             w1_raw[g, 1] = load_float_weight(w1, g, 1)
+        b_picked1 = keep.tile([P, EARLY, PICK], F32, name="b_picked1")
+        for i in range(EARLY):
+            nc.vector.tensor_copy(b_picked1[:, i, :], b_late[i][:].indirect(pick2[:]))
         words1 = [gather_words("words1_%d" % g, table1[g], list1) for g in range(2)]
         w1_q = [
             [quantize("w1_00", round_weight(w1_raw[0, 0], nc.scalar.copy, "a"))],
             [quantize("w1_10", round_weight(w1_raw[1, 0], nc.vector.tensor_copy, "b"))],
         ]
-        d_windows = [ring.tile([P, 2 * S], F32, name="d_windows%d" % n, tag="float_weight%d" % (2 + n)) for n in range(2)]
+        d_windows = [ring.tile([P, 2 * S], F32, name="d_windows%d" % n, tag="float_weight%d" % (2 + n), align_bytes=64) for n in range(2)]
         pick_audiences(1, [slots["a"], slots["b"]], [d_windows[i // 2][:, (i % 2) * S : (i % 2 + 1) * S] for i in range(PACK)])
 
         z_rows0 = keep.tile([P, PACK, PICK], BF16, name="z_rows0", tag="rows2", align_bytes=64)
-        a_rows = [film_rows(0, i) for i in range(PACK)]
+        a_rows = [film_rows(0, i, (0, 1)) for i in range(PACK)]
         w1_q[0].append(quantize("w1_01", round_weight(w1_raw[0, 1], nc.scalar.copy, "c")))
-        for i in range(PACK):
-            if i < PACK - 1:
-                a_picked = scratch()
-            else:
-                a_picked = slots["d"][:, 0:PICK]
-            nc.vector.tensor_copy(a_picked[:], a_rows[i][:].indirect(pick1[:]))
-            gap = scratch()
-            nc.vector.scalar_tensor_tensor(gap[:], a_picked[:], draw_t[:, 0, i : i + 1], b_picked[i][:], ALU.mult, ALU.subtract)
-            join(z_rows0, 0, i, gap, 1.0)
-            if i == 0:
+        a_picked, gaps = {}, {}
+        for step in range(PACK + 2):
+            if step < PACK:
+                a_picked[step] = scratch()[:] if step < PACK - 1 else slots["d"][:, 0:PICK]
+                nc.vector.tensor_copy(a_picked[step], a_rows[step][:].indirect(pick1[:]))
+            if 1 <= step <= PACK:
+                i = step - 1
+                gaps[i] = scratch()
+                nc.vector.scalar_tensor_tensor(
+                    gaps[i][:], a_picked[i], draw_t[:, 0, i : i + 1], b_picked[i], ALU.mult, ALU.subtract
+                )
+                matches[0, i] = tanh(gaps[i], 1.0)
+            if step >= 2:
+                join(z_rows0, 0, step - 2)
+            if step == 0:
                 w1_q[1].append(quantize("w1_11", round_weight(w1_raw[1, 1], nc.scalar.copy, "d")))
 
         w4_packed = load_fp4_words("w4_packed", w4_words, "float_weight1")
         z_rows1 = keep.tile([P, PACK, PICK], BF16, name="z_rows1", tag="rows3", align_bytes=64)
-        a_rows = [film_rows(1, i) for i in range(PACK)]
-        z_q = [weave("z0", z_rows0, nc.scalar.copy, "c")]
-        w4_dealt = (deal_fp4_words("w4_dealt", w4_packed), deal_fp4_planes("w4_dealt_planes", w4_planes))
-        for i in range(PACK):
-            drawn = scratch()
-            nc.vector.tensor_tensor(drawn[:], a_rows[i][:].indirect(pick1[:]), draw_wide[:, i, :], ALU.mult)
-            gap = scratch()
-            nc.vector.tensor_tensor(gap[:], b_late[i][:].indirect(pick2[:]), drawn[:], ALU.subtract)
-            join(z_rows1, 1, i, gap, -1.0)
+        a_rows = [film_rows(1, i, (1, 0)) for i in range(PACK)]
+        w4_dealt_planes = deal_fp4_planes("w4_dealt_planes", w4_planes)
+        drawn = {}
+        for step in range(PACK + 2):
+            if step < PACK:
+                drawn[step] = scratch()
+                if step < EARLY:
+                    nc.vector.tensor_copy(drawn[step][:], a_rows[step][:].indirect(pick1[:]))
+                else:
+                    nc.vector.tensor_tensor(
+                        drawn[step][:], a_rows[step][:].indirect(pick1[:]), draw_wide[:, step - EARLY, :], ALU.mult
+                    )
+            if 1 <= step <= PACK:
+                i = step - 1
+                gaps[i] = scratch()
+                if i < EARLY:
+                    nc.vector.scalar_tensor_tensor(
+                        gaps[i][:], drawn[i][:], draw_t[:, 1, i : i + 1], b_picked1[:, i, :], ALU.mult, ALU.subtract
+                    )
+                    matches[1, i] = tanh(gaps[i], 1.0)
+                else:
+                    nc.vector.tensor_tensor(gaps[i][:], b_late[i][:].indirect(pick2[:]), drawn[i][:], ALU.subtract)
+                    matches[1, i] = tanh(gaps[i], -1.0)
+            if step >= 2:
+                join(z_rows1, 1, step - 2)
+            if step == 1:
+                z_q = [weave("z0", z_rows0, nc.scalar.copy, "c")]
+            if step == 3:
+                w4_dealt = (deal_fp4_words("w4_dealt", w4_packed, "late_window2"), w4_dealt_planes)
         z_q.append(weave("z1", z_rows1, nc.vector.tensor_copy, "d"))
 
         out_rows = out.rearrange("(b p i) j -> b i p j", p=P, i=PACK)

@@ -82,10 +82,10 @@ def tile_list_cinema_week_scores_kernel(
             for r in range(4):
                 queue.dma_start(planes[r:P:32, :, :].bitcast(I32), src[:, r:16:4, :].rearrange("g q n -> q g n").bitcast(I32))
 
-        def deal_fp4_planes(name, planes):
+        def deal_fp4_planes(name, planes, engine):
             passes = planes.shape[1]
             dealt = keep.tile([P, passes, H], U8, name=name, align_bytes=64)
-            nc.vector.tensor_copy(
+            engine.tensor_copy(
                 dealt[:].rearrange("p g (b i m) -> p (g b) i m", b=BLOCKS, i=PACK),
                 planes[:].rearrange("p g (b m i) -> p (g b) i m", b=BLOCKS, i=PACK),
             )
@@ -121,6 +121,9 @@ def tile_list_cinema_week_scores_kernel(
             tile = slots[slot][:].bitcast(BF16)
             copy(tile[:].rearrange("p (i m j) -> p m i j", i=PACK, j=PACK), raw[:].rearrange("p j (m i) -> p m i j", i=PACK))
             return tile
+
+        def round_on_gpsimd(dst, src):
+            nc.gpsimd.tensor_scalar(dst, src, 1.0, 0.0, ALU.mult, ALU.add)
 
         def quantize(name, rounded):
             codes = keep.tile([P, K_PASS], U32, name=name + "_codes", align_bytes=64)
@@ -202,7 +205,7 @@ def tile_list_cinema_week_scores_kernel(
         lim_t = load_channel_vector("lim_t", lim)
 
         words2 = gather_words("words2", table2, list2)
-        w2_dealt = (deal_fp4_words("w2_dealt", w2_packed, "w2_dealt"), deal_fp4_planes("w2_dealt_planes", w2_planes))
+        w2_dealt = (deal_fp4_words("w2_dealt", w2_packed, "w2_dealt"), deal_fp4_planes("w2_dealt_planes", w2_planes, nc.gpsimd))
         w3_q = [quantize("w3_0", round_weight(w3_raw[0], nc.vector.tensor_copy, "e"))]
 
         draw_wide = keep.tile([P, PACK - EARLY, PICK], F32, name="draw_wide")
@@ -246,7 +249,7 @@ def tile_list_cinema_week_scores_kernel(
         d_picked = {}
         b_late = [first_stage(late_window(), fp4_side(w2_dealt, 1, i), [(words2, plane2, 0)]) for i in range(PACK)]
         pick_audiences(0, [keep.tile([P, 2 * PICK], F32, name="d_pair%d" % n) for n in range(2)], [window() for i in range(PACK)])
-        w3_q.append(quantize("w3_1", round_weight(w3_raw[1], nc.scalar.copy, "b")))
+        w3_q.append(quantize("w3_1", round_weight(w3_raw[1], round_on_gpsimd, "b")))
         for g in range(2):
             w1_raw[g, 1] = load_float_weight(w1, g, 1)
         b_picked1 = keep.tile([P, EARLY, PICK], F32, name="b_picked1")
@@ -262,7 +265,7 @@ def tile_list_cinema_week_scores_kernel(
 
         z_rows0 = keep.tile([P, PACK, PICK], BF16, name="z_rows0", tag="rows2", align_bytes=64)
         a_rows = [film_rows(0, i, (0, 1)) for i in range(PACK)]
-        w1_q[0].append(quantize("w1_01", round_weight(w1_raw[0, 1], nc.scalar.copy, "c")))
+        w1_q[0].append(quantize("w1_01", round_weight(w1_raw[0, 1], round_on_gpsimd, "c")))
         a_picked, gaps = {}, {}
         for step in range(PACK + 2):
             if step < PACK:
@@ -283,7 +286,7 @@ def tile_list_cinema_week_scores_kernel(
         w4_packed = load_fp4_words("w4_packed", w4_words, "float_weight1")
         z_rows1 = keep.tile([P, PACK, PICK], BF16, name="z_rows1", tag="rows3", align_bytes=64)
         a_rows = [film_rows(1, i, (1, 0)) for i in range(PACK)]
-        w4_dealt_planes = deal_fp4_planes("w4_dealt_planes", w4_planes)
+        w4_dealt_planes = deal_fp4_planes("w4_dealt_planes", w4_planes, nc.gpsimd)
         drawn = {}
         for step in range(PACK + 2):
             if step < PACK:

@@ -34,6 +34,7 @@ def tile_list_cinema_week_scores_kernel(
         lists = ctx.enter_context(tc.tile_pool(name="lists", bufs=1))
         keep = ctx.enter_context(tc.tile_pool(name="keep", bufs=1))
         ring = ctx.enter_context(tc.tile_pool(name="ring", bufs=1))
+        overlay = ctx.enter_context(tc.tile_pool(name="overlay", bufs=1))
         psum = ctx.enter_context(tc.psum_pool(name="psum", bufs=1))
 
         def turns(pool, name, count, shape, dtype, align=64):
@@ -50,7 +51,8 @@ def tile_list_cinema_week_scores_kernel(
         late_window = turns(ring, "late_window", 4, [P, S], F32)
         scratch = turns(ring, "scratch", 8, [P, PICK], F32)
         float_weight = turns(ring, "float_weight", 4, [P, PACK, K_PASS], F32)
-        slots = {name: ring.tile([P, 2 * PICK], F32, name="slot_" + name, align_bytes=64) for name in "abcde"}
+        slots = {name: ring.tile([P, 2 * PICK], F32, name="slot_" + name, align_bytes=64) for name in "acde"}
+        slots["b"] = overlay.tile([P, 2 * PICK], F32, name="slot_b", align_bytes=64, offset=0)
 
         def load_list(name, src):
             tile = lists.tile([P, src.shape[1]], U16, name=name)
@@ -82,9 +84,7 @@ def tile_list_cinema_week_scores_kernel(
             for r in range(4):
                 queue.dma_start(planes[r:P:32, :, :].bitcast(I32), src[:, r:16:4, :].rearrange("g q n -> q g n").bitcast(I32))
 
-        def deal_fp4_planes(name, planes, engine):
-            passes = planes.shape[1]
-            dealt = keep.tile([P, passes, H], U8, name=name, align_bytes=64)
+        def deal_fp4_planes(dealt, planes, engine):
             engine.tensor_copy(
                 dealt[:].rearrange("p g (b i m) -> p (g b) i m", b=BLOCKS, i=PACK),
                 planes[:].rearrange("p g (b m i) -> p (g b) i m", b=BLOCKS, i=PACK),
@@ -121,9 +121,6 @@ def tile_list_cinema_week_scores_kernel(
             tile = slots[slot][:].bitcast(BF16)
             copy(tile[:].rearrange("p (i m j) -> p m i j", i=PACK, j=PACK), raw[:].rearrange("p j (m i) -> p m i j", i=PACK))
             return tile
-
-        def round_on_gpsimd(dst, src):
-            nc.gpsimd.tensor_scalar(dst, src, 1.0, 0.0, ALU.mult, ALU.add)
 
         def quantize(name, rounded):
             codes = keep.tile([P, K_PASS], U32, name=name + "_codes", align_bytes=64)
@@ -205,18 +202,17 @@ def tile_list_cinema_week_scores_kernel(
         lim_t = load_channel_vector("lim_t", lim)
 
         words2 = gather_words("words2", table2, list2)
-        w2_dealt = (deal_fp4_words("w2_dealt", w2_packed, "w2_dealt"), deal_fp4_planes("w2_dealt_planes", w2_planes, nc.gpsimd))
+        w2_dealt = (deal_fp4_words("w2_dealt", w2_packed, "w2_dealt"), deal_fp4_planes(keep.tile([P, 1, H], U8, name="w2_dealt_planes", align_bytes=64), w2_planes, nc.gpsimd))
         w3_q = [quantize("w3_0", round_weight(w3_raw[0], nc.vector.tensor_copy, "e"))]
 
         draw_wide = keep.tile([P, PACK - EARLY, PICK], F32, name="draw_wide")
         nc.scalar.copy(draw_wide[:], draw_t[:, 1, EARLY:].unsqueeze(2).to_broadcast([P, PACK - EARLY, PICK]))
 
-        def pick_audiences(blk, pairs, windows):
-            for half, pair in enumerate(pairs):
-                for e in range(2):
-                    d_rows = first_stage(windows[2 * half + e], fp8_side([w3_q], blk, 2 * half + e), [(words3, plane3, 0)])
-                    nc.vector.tensor_copy(pair[:, e * PICK : (e + 1) * PICK], d_rows[:].indirect(pick3[:]))
-                    d_picked[blk, 2 * half + e] = pair[:, e * PICK : (e + 1) * PICK]
+        def pick_audiences(blk, places, windows):
+            for i in range(PACK):
+                d_rows = first_stage(windows[i], fp8_side([w3_q], blk, i), [(words3, plane3, 0)])
+                nc.vector.tensor_copy(places[i], d_rows[:].indirect(pick3[:]))
+                d_picked[blk, i] = places[i]
 
         def film_rows(blk, i, passes):
             return first_stage(
@@ -248,8 +244,8 @@ def tile_list_cinema_week_scores_kernel(
             nc.vector.tensor_copy(b_picked[i], b_rows[i][:].indirect(pick2[:]))
         d_picked = {}
         b_late = [first_stage(late_window(), fp4_side(w2_dealt, 1, i), [(words2, plane2, 0)]) for i in range(PACK)]
-        pick_audiences(0, [keep.tile([P, 2 * PICK], F32, name="d_pair%d" % n) for n in range(2)], [window() for i in range(PACK)])
-        w3_q.append(quantize("w3_1", round_weight(w3_raw[1], round_on_gpsimd, "b")))
+        pick_audiences(0, [keep.tile([P, PICK], F32, name="d_picked%d" % i)[:] for i in range(PACK)], [window() for i in range(PACK)])
+        w3_q.append(quantize("w3_1", round_weight(w3_raw[1], nc.scalar.copy, "b")))
         for g in range(2):
             w1_raw[g, 1] = load_float_weight(w1, g, 1)
         b_picked1 = keep.tile([P, EARLY, PICK], F32, name="b_picked1")
@@ -260,12 +256,17 @@ def tile_list_cinema_week_scores_kernel(
             [quantize("w1_00", round_weight(w1_raw[0, 0], nc.scalar.copy, "a"))],
             [quantize("w1_10", round_weight(w1_raw[1, 0], nc.vector.tensor_copy, "b"))],
         ]
-        d_windows = [ring.tile([P, 2 * S], F32, name="d_windows%d" % n, tag="float_weight%d" % (2 + n), align_bytes=64) for n in range(2)]
-        pick_audiences(1, [slots["a"], slots["b"]], [d_windows[i // 2][:, (i % 2) * S : (i % 2 + 1) * S] for i in range(PACK)])
+        d_windows = ring.tile([P, PACK * S], F32, name="d_windows", tag="float_weight2", align_bytes=64)
+        w4_dealt_planes = deal_fp4_planes(
+            overlay.tile([P, 2, H], U8, name="w4_dealt_planes", align_bytes=64, offset=4 * PICK), w4_planes, nc.gpsimd
+        )
+        d_held = overlay.tile([P, PICK], F32, name="d_held", align_bytes=64, offset=0)
+        d_last = keep.tile([P, PICK], F32, name="d_last")
+        pick_audiences(1, [d_last[:], slots["a"][:, 0:PICK], slots["a"][:, PICK : 2 * PICK], d_held[:]], [d_windows[:, i * S : (i + 1) * S] for i in range(PACK)])
 
         z_rows0 = keep.tile([P, PACK, PICK], BF16, name="z_rows0", tag="rows2", align_bytes=64)
         a_rows = [film_rows(0, i, (0, 1)) for i in range(PACK)]
-        w1_q[0].append(quantize("w1_01", round_weight(w1_raw[0, 1], round_on_gpsimd, "c")))
+        w1_q[0].append(quantize("w1_01", round_weight(w1_raw[0, 1], nc.scalar.copy, "c")))
         a_picked, gaps = {}, {}
         for step in range(PACK + 2):
             if step < PACK:
@@ -286,7 +287,6 @@ def tile_list_cinema_week_scores_kernel(
         w4_packed = load_fp4_words("w4_packed", w4_words, "float_weight1")
         z_rows1 = keep.tile([P, PACK, PICK], BF16, name="z_rows1", tag="rows3", align_bytes=64)
         a_rows = [film_rows(1, i, (1, 0)) for i in range(PACK)]
-        w4_dealt_planes = deal_fp4_planes("w4_dealt_planes", w4_planes, nc.gpsimd)
         drawn = {}
         for step in range(PACK + 2):
             if step < PACK:

from contextlib import ExitStack

import concourse.mybir as mybir

K, K2, H, T, S, PICK = 1024, 512, 1024, 4096, 1024, 512
FLOPS = 2 * H * S * (K + K2 + K2) + 2 * H * H * PICK

F32 = mybir.dt.float32
BF16 = mybir.dt.bfloat16
I32 = mybir.dt.int32
U32 = mybir.dt.uint32
U16 = mybir.dt.uint16
U8 = mybir.dt.uint8
FP8X4 = mybir.dt.float8_e4m3fn_x4
FP4X4 = mybir.dt.float4_e2m1fn_x4
ALU = mybir.AluOpType
ACT = mybir.ActivationFunctionType

P = 128
PACK = 4
K_PASS = P * PACK
BANK = 512
BLOCKS = H // K_PASS
EARLY = 2
ROW_TILES = [(blk, i) for blk in range(BLOCKS) for i in range(PACK)]


def tile_list_cinema_week_scores_kernel(
    tc, tab_words, tab_scales, tab2_words, tab2_scales, tab3_words, tab3_scales, offs, offs2, offs3,
    pos1, pos2, pos3, w1, w2_words, w2_scales, w3, w4_words, w4_scales, draw, fit, lim, out,
):
    nc = tc.nc
    with ExitStack() as ctx:
        lists = ctx.enter_context(tc.tile_pool(name="lists", bufs=1))
        keep = ctx.enter_context(tc.tile_pool(name="keep", bufs=1))
        ring = ctx.enter_context(tc.tile_pool(name="ring", bufs=1))
        overlay = ctx.enter_context(tc.tile_pool(name="overlay", bufs=1))
        psum = ctx.enter_context(tc.psum_pool(name="psum", bufs=1))

        def turns(pool, name, count, shape, dtype, align=64):
            tiles = [pool.tile(shape, dtype, name="%s%d" % (name, n), tag="%s%d" % (name, n), align_bytes=align) for n in range(count)]

            def take():
                tiles.append(tiles.pop(0))
                return tiles[-1]

            return take

        bank = turns(psum, "bank", 8, [P, BANK], F32, None)
        window = turns(ring, "window", 4, [P, S], F32)
        late_window = turns(ring, "late_window", 4, [P, S], F32)
        scratch = turns(ring, "scratch", 8, [P, PICK], F32)
        float_weight = turns(ring, "float_weight", 4, [P, PACK, K_PASS], F32)
        slots = {name: ring.tile([P, 2 * PICK], F32, name="slot_" + name, align_bytes=64) for name in "acde"}
        slots["b"] = overlay.tile([P, 2 * PICK], F32, name="slot_b", align_bytes=64, offset=0)

        def load_list(name, src):
            tile = lists.tile([P, src.shape[1]], U16, name=name)
            nc.sync.dma_start(tile[:], src)
            return tile

        def load_channel_vector(name, src):
            tile = keep.tile([P, BLOCKS, PACK], F32, name=name)
            nc.sync.dma_start(tile[:], src.rearrange("(b p i) -> p b i", p=P, i=PACK))
            return tile

        def zeroed_bytes(name, shape, engine, partitions=P):
            tile = keep.tile(shape, U8, name=name, tag=name, align_bytes=64)
            engine.memset(tile[0:partitions].bitcast(I32), 0)
            return tile

        def load_scale_rows(tile, src, first):
            rows = src.rearrange("g q n -> (g q) n")
            nc.sync.dma_start(tile[first : first + rows.shape[0], :].bitcast(I32), rows.bitcast(I32))

        def place_scale_rows(plane, rows, first_row, first_partition=0):
            for r in range(4):
                nc.sync.dma_start(
                    plane[first_partition + r : P : 32, :].bitcast(I32),
                    rows[first_row + r : first_row + 16 : 4, :].bitcast(I32),
                )

        def load_planes(planes, src, queue):
            for r in range(4):
                queue.dma_start(planes[r:P:32, :, :].bitcast(I32), src[:, r:16:4, :].rearrange("g q n -> q g n").bitcast(I32))

        def deal_fp4_planes(dealt, planes, engine):
            engine.tensor_copy(
                dealt[:].rearrange("p g (b i m) -> p (g b) i m", b=BLOCKS, i=PACK),
                planes[:].rearrange("p g (b m i) -> p (g b) i m", b=BLOCKS, i=PACK),
            )
            return dealt

        def load_table_words(name, src, tag):
            tile = ring.tile([P, T], I32, name=name, tag=tag)
            nc.sync.dma_start(tile[:], src.rearrange("p n i -> p (n i)").bitcast(I32))
            return tile

        def load_fp4_words(name, src, tag):
            tile = ring.tile([P, src.shape[0], H // 2], I32, name=name, tag=tag, align_bytes=64)
            nc.sync.dma_start(tile[:], src.rearrange("g p n -> p g n").bitcast(I32))
            return tile

        def load_float_weight(w, g, blk):
            tile = float_weight()
            rows = w[g * K_PASS : (g + 1) * K_PASS, blk * K_PASS : (blk + 1) * K_PASS]
            nc.sync.dma_start(tile[:], rows.rearrange("(p j) c -> p j c", j=PACK))
            return tile

        def gather_words(name, table, offsets):
            tile = keep.tile([P, S], U32, name=name, align_bytes=64)
            nc.vector.tensor_copy(tile[:], table[:].bitcast(U32).indirect(offsets[:]))
            return tile

        def gather_scales(name, plane, offsets):
            tile = keep.tile([P, S], U8, name=name, align_bytes=64)
            nc.vector.tensor_copy(tile[:], plane[:].indirect(offsets[:]))
            return tile

        def round_weight(raw, copy, slot):
            tile = slots[slot][:].bitcast(BF16)
            copy(tile[:].rearrange("p (i m j) -> p m i j", i=PACK, j=PACK), raw[:].rearrange("p j (m i) -> p m i j", i=PACK))
            return tile

        def quantize(name, rounded):
            codes = keep.tile([P, K_PASS], U32, name=name + "_codes", align_bytes=64)
            scales = keep.tile([P, K_PASS], U8, name=name + "_scales", align_bytes=64)
            nc.vector.quantize_mx(out=codes[:].bitcast(FP8X4), scales=scales[:], in_=rounded[:])
            return codes, scales

        def deal_fp4_words(name, words, tag):
            passes = words.shape[1]
            dealt = ring.tile([P, passes, 2 * H], U8, name=name, tag=tag, align_bytes=64)
            for g in range(passes):
                nc.scalar.copy(
                    dealt[:, g, :].bitcast(U16).rearrange("p (b i m) -> p b i m", b=BLOCKS, i=PACK),
                    words[:, g, :].bitcast(U16).rearrange("p (b m i) -> p b i m", b=BLOCKS, i=PACK),
                )
            return dealt

        def fp8_side(quantized, blk, i):
            cols = slice(i * P, (i + 1) * P)
            return [(q[blk][0][:, cols].bitcast(FP8X4), q[blk][1][:, cols]) for q in quantized]

        def fp4_side(dealt, blk, i):
            c0 = blk * K_PASS + i * P
            return [
                (dealt[0][:, g, 2 * c0 : 2 * (c0 + P)].bitcast(FP4X4), dealt[1][:, g, c0 : c0 + P])
                for g in range(dealt[0].shape[1])
            ]

        def first_stage(rows, stationary, moving):
            for c0 in range(0, S, BANK):
                acc = bank()
                for g, ((w_codes, w_scales), (v_words, v_plane, first)) in enumerate(zip(stationary, moving)):
                    nc.tensor.matmul_mx(
                        out=acc[:], lhsT=w_codes, lhsT_scale=w_scales,
                        rhs=v_words[:, c0 : c0 + BANK].bitcast(FP8X4), rhs_scale=v_plane[first:P, c0 : c0 + BANK],
                        start=(g == 0), stop=(g == len(moving) - 1),
                    )
                nc.scalar.copy(rows[:, c0 : c0 + BANK], acc[:])
            return rows

        w2_planes = zeroed_bytes("w2_planes", [P, 1, H], nc.vector)
        rows2 = zeroed_bytes("rows2", [P, T], nc.vector, P - 16)
        rows3 = zeroed_bytes("rows3", [P, T], nc.vector, P - 16)
        rows1 = zeroed_bytes("rows1", [P, T], nc.gpsimd, P - 32)
        plane1 = zeroed_bytes("plane1", [P, S], nc.gpsimd)
        planes23 = zeroed_bytes("planes23", [P, 2 * S], nc.gpsimd)
        w4_planes = zeroed_bytes("w4_planes", [P, 2, H], nc.gpsimd)

        list2 = load_list("list2", offs2)
        load_scale_rows(rows2, tab2_scales, P - 16)
        list3 = load_list("list3", offs3)
        load_scale_rows(rows3, tab3_scales, P - 16)
        list1 = load_list("list1", offs)
        load_scale_rows(rows1, tab_scales, P - 32)
        w2_packed = load_fp4_words("w2_packed", w2_words, "w2_packed")
        table2 = load_table_words("table2", tab2_words[0], "table_a")
        load_planes(w2_planes, w2_scales, nc.sync)
        draw_t = load_channel_vector("draw_t", draw)
        w3_raw = [load_float_weight(w3, 0, 0)]
        pick2 = load_list("pick2", pos2)

        picked23 = keep.tile([P, 2 * S], U8, name="picked23")
        nc.vector.tensor_copy(picked23[:, 0:S], rows2[:].indirect(list2[:]))
        nc.vector.tensor_copy(picked23[:, S : 2 * S], rows3[:].indirect(list3[:]))
        place_scale_rows(planes23, picked23, P - 16)
        plane2, plane3 = planes23[:, 0:S], planes23[:, S : 2 * S]
        picked1 = gather_scales("picked1", rows1, list1)
        table3 = load_table_words("table3", tab3_words[0], "table_b")
        pick3 = load_list("pick3", pos3)
        w3_raw.append(load_float_weight(w3, 0, 1))
        place_scale_rows(plane1, picked1, P - 32)
        table1 = [load_table_words("table1_0", tab_words[0], "table_c")]
        place_scale_rows(plane1, picked1, P - 16, 4)
        table1.append(load_table_words("table1_1", tab_words[1], "table_a"))
        w1_raw = {(g, 0): load_float_weight(w1, g, 0) for g in range(2)}
        pick1 = load_list("pick1", pos1)
        fit_t = load_channel_vector("fit_t", fit)
        load_planes(w4_planes, w4_scales, nc.sync)
        lim_t = load_channel_vector("lim_t", lim)

        words2 = gather_words("words2", table2, list2)
        w2_dealt = (deal_fp4_words("w2_dealt", w2_packed, "w2_dealt"), deal_fp4_planes(keep.tile([P, 1, H], U8, name="w2_dealt_planes", align_bytes=64), w2_planes, nc.gpsimd))
        w3_q = [quantize("w3_0", round_weight(w3_raw[0], nc.vector.tensor_copy, "e"))]

        draw_wide = keep.tile([P, PACK - EARLY, PICK], F32, name="draw_wide")
        nc.scalar.copy(draw_wide[:], draw_t[:, 1, EARLY:].unsqueeze(2).to_broadcast([P, PACK - EARLY, PICK]))

        def pick_audiences(blk, places, windows):
            for i in range(PACK):
                d_rows = first_stage(windows[i], fp8_side([w3_q], blk, i), [(words3, plane3, 0)])
                nc.vector.tensor_copy(places[i], d_rows[:].indirect(pick3[:]))
                d_picked[blk, i] = places[i]

        def film_rows(blk, i, passes):
            return first_stage(
                window(), fp8_side([w1_q[g] for g in passes], blk, i), [(words1[g], plane1, 4 * g) for g in passes]
            )

        matches = {}

        def tanh(gap, sign):
            match = scratch()
            nc.scalar.activation(match[:], gap[:], ACT.Tanh, scale=sign)
            return match

        def join(z_rows, blk, i):
            nc.vector.scalar_tensor_tensor(
                z_rows[:, i, :], matches[blk, i][:], fit_t[:, blk, i : i + 1], d_picked[blk, i], ALU.mult, ALU.add
            )

        def weave(name, z_rows, copy, slot):
            z_woven = slots[slot][:].bitcast(BF16)
            copy(z_woven[:].rearrange("p (c e i) -> p c i e", e=4, i=PACK), z_rows[:].rearrange("p i (c e) -> p c i e", e=4))
            return quantize(name, z_woven)

        b_rows = [first_stage(window(), fp4_side(w2_dealt, 0, i), [(words2, plane2, 0)]) for i in range(PACK)]
        words3 = gather_words("words3", table3, list3)
        b_pairs = [slots["e"], ring.tile([P, 2 * PICK], F32, name="b_pair", tag="table_b")]
        b_picked = [b_pairs[i // 2][:, (i % 2) * PICK : (i % 2 + 1) * PICK] for i in range(PACK)]
        for i in range(PACK):
            nc.vector.tensor_copy(b_picked[i], b_rows[i][:].indirect(pick2[:]))
        d_picked = {}
        b_late = [first_stage(late_window(), fp4_side(w2_dealt, 1, i), [(words2, plane2, 0)]) for i in range(PACK)]
        pick_audiences(0, [keep.tile([P, PICK], F32, name="d_picked%d" % i)[:] for i in range(PACK)], [window() for i in range(PACK)])
        w3_q.append(quantize("w3_1", round_weight(w3_raw[1], nc.scalar.copy, "b")))
        for g in range(2):
            w1_raw[g, 1] = load_float_weight(w1, g, 1)
        b_picked1 = keep.tile([P, EARLY, PICK], F32, name="b_picked1")
        for i in range(EARLY):
            nc.vector.tensor_copy(b_picked1[:, i, :], b_late[i][:].indirect(pick2[:]))
        words1 = [gather_words("words1_%d" % g, table1[g], list1) for g in range(2)]
        w1_q = [
            [quantize("w1_00", round_weight(w1_raw[0, 0], nc.scalar.copy, "a"))],
            [quantize("w1_10", round_weight(w1_raw[1, 0], nc.vector.tensor_copy, "b"))],
        ]
        d_windows = ring.tile([P, PACK * S], F32, name="d_windows", tag="float_weight2", align_bytes=64)
        w4_dealt_planes = deal_fp4_planes(
            overlay.tile([P, 2, H], U8, name="w4_dealt_planes", align_bytes=64, offset=4 * PICK), w4_planes, nc.gpsimd
        )
        d_held = overlay.tile([P, PICK], F32, name="d_held", align_bytes=64, offset=0)
        d_last = keep.tile([P, PICK], F32, name="d_last")
        pick_audiences(1, [d_last[:], slots["a"][:, 0:PICK], slots["a"][:, PICK : 2 * PICK], d_held[:]], [d_windows[:, i * S : (i + 1) * S] for i in range(PACK)])

        z_rows0 = keep.tile([P, PACK, PICK], BF16, name="z_rows0", tag="rows2", align_bytes=64)
        a_rows = [film_rows(0, i, (0, 1)) for i in range(PACK)]
        w1_q[0].append(quantize("w1_01", round_weight(w1_raw[0, 1], nc.scalar.copy, "c")))
        a_picked, gaps = {}, {}
        for step in range(PACK + 2):
            if step < PACK:
                a_picked[step] = scratch()[:] if step < PACK - 1 else slots["d"][:, 0:PICK]
                nc.vector.tensor_copy(a_picked[step], a_rows[step][:].indirect(pick1[:]))
            if 1 <= step <= PACK:
                i = step - 1
                gaps[i] = scratch()
                nc.vector.scalar_tensor_tensor(
                    gaps[i][:], a_picked[i], draw_t[:, 0, i : i + 1], b_picked[i], ALU.mult, ALU.subtract
                )
                matches[0, i] = tanh(gaps[i], 1.0)
            if step >= 2:
                join(z_rows0, 0, step - 2)
            if step == 0:
                w1_q[1].append(quantize("w1_11", round_weight(w1_raw[1, 1], nc.scalar.copy, "d")))

        w4_packed = load_fp4_words("w4_packed", w4_words, "float_weight1")
        z_rows1 = keep.tile([P, PACK, PICK], BF16, name="z_rows1", tag="rows3", align_bytes=64)
        a_rows = [film_rows(1, i, (1, 0)) for i in range(PACK)]
        drawn = {}
        for step in range(PACK + 2):
            if step < PACK:
                drawn[step] = scratch()
                if step < EARLY:
                    nc.vector.tensor_copy(drawn[step][:], a_rows[step][:].indirect(pick1[:]))
                else:
                    nc.vector.tensor_tensor(
                        drawn[step][:], a_rows[step][:].indirect(pick1[:]), draw_wide[:, step - EARLY, :], ALU.mult
                    )
            if 1 <= step <= PACK:
                i = step - 1
                gaps[i] = scratch()
                if i < EARLY:
                    nc.vector.scalar_tensor_tensor(
                        gaps[i][:], drawn[i][:], draw_t[:, 1, i : i + 1], b_picked1[:, i, :], ALU.mult, ALU.subtract
                    )
                    matches[1, i] = tanh(gaps[i], 1.0)
                else:
                    nc.vector.tensor_tensor(gaps[i][:], b_late[i][:].indirect(pick2[:]), drawn[i][:], ALU.subtract)
                    matches[1, i] = tanh(gaps[i], -1.0)
            if step >= 2:
                join(z_rows1, 1, step - 2)
            if step == 1:
                z_q = [weave("z0", z_rows0, nc.scalar.copy, "c")]
            if step == 3:
                w4_dealt = (deal_fp4_words("w4_dealt", w4_packed, "late_window2"), w4_dealt_planes)
        z_q.append(weave("z1", z_rows1, nc.vector.tensor_copy, "d"))

        out_rows = out.rearrange("(b p i) j -> b i p j", p=P, i=PACK)
        y_acc = {key: bank() for key in ROW_TILES}
        for g in range(BLOCKS):
            for blk, i in ROW_TILES:
                w_codes, w_scales = fp4_side(w4_dealt, blk, i)[g]
                nc.tensor.matmul_mx(
                    out=y_acc[blk, i][:], lhsT=w_codes, lhsT_scale=w_scales,
                    rhs=z_q[g][0][:].bitcast(FP8X4), rhs_scale=z_q[g][1][:], start=(g == 0), stop=(g == BLOCKS - 1),
                )
        for blk, i in ROW_TILES:
            limited = scratch()
            nc.vector.scalar_tensor_tensor(
                limited[:], d_picked[blk, i], lim_t[:, blk, i : i + 1], y_acc[blk, i][:], ALU.mult, ALU.min
            )
            nc.sync.dma_start(out_rows[blk, i], limited[:])
